import numpy as np
CORES = [1,2,9,10,17,18,25,26,33,34,41,42,49,50,57,58,65,66,73,74,81,82,89,90,97,98,105,106,113,114,121,122]
N = 32
GROUPS = [[0,1,4,5,8,9,12,13,16,17,20,21,24,25,28,29],[2,3,6,7,10,11,14,15,18,19,22,23,26,27,30,31]]
def setup_inputs(rng):
    return {"x": rng.standard_normal((N, 128, 128), dtype=np.float32)}
def reference(x):
    y = np.empty((N, 128, 128), x.dtype)
    for g in GROUPS:
        s = x[g].sum(axis=0, dtype=np.float64).astype(x[g].dtype)
        for r in g:
            y[r] = s
    return {"y": y}

@@ -1,0 +1,91 @@
+from concourse.bass import DstId, RemoteDMATransfer
+
+UNITS = 16
+SCRATCH = {
+    "xs":  ("dram", [UNITS, 128, 8], "float32"),
+    "pa":  ("dram", [UNITS, 128, 8], "float32"),
+    "pb":  ("dram", [UNITS, 128, 8], "float32"),
+    "rs":  ("dram", [8, 128, 8], "float32"),
+    "res": ("dram", [UNITS, 128, 8], "float32"),
+}
+SEMAPHORES = ["loaded", "stored", "s1", "s2", "s3", "s4", "sent"]
+
+HELP_SENDERS = (5, 6)
+REDUCER = (0, 4)
+
+
+def rank_program(g, core, T, topo):
+    ch, k = topo.chip(core), core % 8
+    group = None
+    for members in T.tables["GROUPS"]:
+        cs = [T.cores[r] for r in members]
+        if ch in [topo.chip(c) for c in cs]:
+            group = cs
+    if group is None:
+        return
+    chips = sorted(set(topo.chip(c) for c in group))
+    me = chips.index(ch)
+    ranks = sorted(c % 8 for c in group if topo.chip(c) == ch)
+    assert len(chips) == 8 and len(ranks) == 2
+
+    def did(c):
+        rid, pid, _se = topo.addr(c)
+        return DstId(rid=rid, pnc=pid)
+
+    def sender(u):
+        h, j = divmod(u, 8)
+        return (ranks if h == 0 else HELP_SENDERS)[j // 4]
+
+    sent = 0
+    is_rank = k in ranks
+
+    if is_rank:
+        g.dma_start(T.xs[:], T.x[:]).then_inc(T.sem.loaded, 16)
+        g.wait_ge(T.sem.loaded, 16)
+        land = T.pa if k == ranks[0] else T.pb
+        away = [u for u in range(UNITS) if sender(u) != k]
+        g.remote_dma_fused(
+            [RemoteDMATransfer(dst_ids=[did(ch * 8 + sender(u))], dma_engine_mask=1 << e, remote_sem=T.sem.s1,
+                               src=T.xs[u], dst=land[u]) for e, u in enumerate(away)],
+            local_sem=T.sem.sent)
+        sent += len(away)
+
+    mine = [u for u in range(UNITS) if sender(u) == k]
+    if mine:
+        g.wait_ge(T.sem.s1, 4 if is_rank else 8)
+        trs = []
+        for e, u in enumerate(mine):
+            h, j = divmod(u, 8)
+            a = T.xs[u] if k == ranks[0] else T.pa[u]
+            b = T.xs[u] if k == ranks[1] else T.pb[u]
+            trs.append(RemoteDMATransfer(dst_ids=[did(chips[j] * 8 + REDUCER[h])], dma_engine_mask=3 << (2 * e),
+                                         remote_sem=T.sem.s2, srcs=[a, b], dsts=[T.rs[me]], alu_op=1))
+        g.remote_dma_fused(trs, local_sem=T.sem.sent)
+        sent += 2 * len(mine)
+
+    if k in REDUCER:
+        h = REDUCER.index(k)
+        u = 8 * h + me
+        g.wait_ge(T.sem.s2, 16)
+        g.remote_dma_fused(
+            [RemoteDMATransfer(dst_ids=[did(c * 8 + ranks[h]) for c in chips], dma_engine_mask=0xFF,
+                               remote_sem=T.sem.s3, srcs=[T.rs[i] for i in range(8)],
+                               dsts=[T.res[u] for c in chips], alu_op=1)],
+            local_sem=T.sem.sent)
+        sent += 8
+
+    if is_rank:
+        h = ranks.index(k)
+        other = ch * 8 + ranks[1 - h]
+        g.wait_ge(T.sem.s3, 64)
+        g.remote_dma_fused(
+            [RemoteDMATransfer(dst_ids=[did(other)], dma_engine_mask=3 << (2 * j), remote_sem=T.sem.s4,
+                               src=T.res[8 * h + j], dst=T.res[8 * h + j]) for j in range(8)],
+            local_sem=T.sem.sent)
+        sent += 16
+        g.wait_ge(T.sem.s4, 16)
+        g.dma_start(T.y[:], T.res[:]).then_inc(T.sem.stored, 16)
+        g.wait_ge(T.sem.stored, 16)
+
+    if sent:
+        g.wait_ge(T.sem.sent, sent)

@@ -6,12 +6,13 @@ SCRATCH = {
     "pa":  ("dram", [UNITS, 128, 8], "float32"),
     "pb":  ("dram", [UNITS, 128, 8], "float32"),
     "rs":  ("dram", [8, 128, 8], "float32"),
+    "ag":  ("dram", [8, 128, 8], "float32"),
     "res": ("dram", [UNITS, 128, 8], "float32"),
 }
 SEMAPHORES = ["loaded", "stored", "s1", "s2", "s3", "s4", "sent"]
 
-HELP_SENDERS = (5, 6)
-REDUCER = (0, 4)
+PAIR = ((0, 3), (5, 6))
+RELAY = (7, 4)
 
 
 def rank_program(g, core, T, topo):
@@ -27,65 +28,62 @@ def rank_program(g, core, T, topo):
     me = chips.index(ch)
     ranks = sorted(c % 8 for c in group if topo.chip(c) == ch)
     assert len(chips) == 8 and len(ranks) == 2
+    assert not set(ranks) & set(PAIR[0] + PAIR[1] + RELAY)
 
-    def did(c):
-        rid, pid, _se = topo.addr(c)
+    def did(chip_, k_):
+        rid, pid, _se = topo.addr(chip_ * 8 + k_)
         return DstId(rid=rid, pnc=pid)
 
     def sender(u):
         h, j = divmod(u, 8)
-        return (ranks if h == 0 else HELP_SENDERS)[j // 4]
+        return PAIR[h][j // 4]
 
-    sent = 0
-    is_rank = k in ranks
+    def reducer(u):
+        h, j = divmod(u, 8)
+        return PAIR[h][1 - j // 4]
 
-    if is_rank:
-        g.dma_start(T.xs[:], T.x[:]).then_inc(T.sem.loaded, 16)
+    if k in ranks:
+        g.sync.dma_start(T.xs[:], T.x[:]).then_inc(T.sem.loaded, 16)
         g.wait_ge(T.sem.loaded, 16)
         land = T.pa if k == ranks[0] else T.pb
-        away = [u for u in range(UNITS) if sender(u) != k]
         g.remote_dma_fused(
-            [RemoteDMATransfer(dst_ids=[did(ch * 8 + sender(u))], dma_engine_mask=1 << e, remote_sem=T.sem.s1,
-                               src=T.xs[u], dst=land[u]) for e, u in enumerate(away)],
+            [RemoteDMATransfer(dst_ids=[did(ch, sender(u))], dma_engine_mask=1 << u, remote_sem=T.sem.s1,
+                               src=T.xs[u], dst=land[u]) for u in range(UNITS)],
             local_sem=T.sem.sent)
-        sent += len(away)
+        g.sync.wait_ge(T.sem.s4, 32)
+        g.sync.dma_start(T.y[:], T.res[:]).then_inc(T.sem.stored, 16)
+        g.wait_ge(T.sem.sent, 16)
+        g.wait_ge(T.sem.stored, 16)
+        return
 
-    mine = [u for u in range(UNITS) if sender(u) == k]
-    if mine:
-        g.wait_ge(T.sem.s1, 4 if is_rank else 8)
-        trs = []
-        for e, u in enumerate(mine):
-            h, j = divmod(u, 8)
-            a = T.xs[u] if k == ranks[0] else T.pa[u]
-            b = T.xs[u] if k == ranks[1] else T.pb[u]
-            trs.append(RemoteDMATransfer(dst_ids=[did(chips[j] * 8 + REDUCER[h])], dma_engine_mask=3 << (2 * e),
-                                         remote_sem=T.sem.s2, srcs=[a, b], dsts=[T.rs[me]], alu_op=1))
-        g.remote_dma_fused(trs, local_sem=T.sem.sent)
-        sent += 2 * len(mine)
-
-    if k in REDUCER:
-        h = REDUCER.index(k)
-        u = 8 * h + me
-        g.wait_ge(T.sem.s2, 16)
+    if k in PAIR[0] + PAIR[1]:
+        mine = [u for u in range(UNITS) if sender(u) == k]
+        g.wait_ge(T.sem.s1, 8)
         g.remote_dma_fused(
-            [RemoteDMATransfer(dst_ids=[did(c * 8 + ranks[h]) for c in chips], dma_engine_mask=0xFF,
-                               remote_sem=T.sem.s3, srcs=[T.rs[i] for i in range(8)],
-                               dsts=[T.res[u] for c in chips], alu_op=1)],
+            [RemoteDMATransfer(dst_ids=[did(chips[u % 8], reducer(u))], dma_engine_mask=3 << (2 * e),
+                               remote_sem=T.sem.s2, srcs=[T.pa[u], T.pb[u]], dsts=[T.rs[me]], alu_op=1)
+             for e, u in enumerate(mine)],
             local_sem=T.sem.sent)
-        sent += 8
+        sent = 8
+        red = [u for u in range(UNITS) if u % 8 == me and reducer(u) == k]
+        for u in red:
+            h = u // 8
+            g.wait_ge(T.sem.s2, 16)
+            g.remote_dma_fused(
+                [RemoteDMATransfer(dst_ids=[did(c, RELAY[h]) for c in chips], dma_engine_mask=0xFF,
+                                   remote_sem=T.sem.s3, srcs=[T.rs[i] for i in range(8)],
+                                   dsts=[T.ag[me] for c in chips], alu_op=1)],
+                local_sem=T.sem.sent)
+            sent += 8
+        g.wait_ge(T.sem.sent, sent)
+        return
 
-    if is_rank:
-        h = ranks.index(k)
-        other = ch * 8 + ranks[1 - h]
+    if k in RELAY:
+        h = RELAY.index(k)
         g.wait_ge(T.sem.s3, 64)
         g.remote_dma_fused(
-            [RemoteDMATransfer(dst_ids=[did(other)], dma_engine_mask=3 << (2 * j), remote_sem=T.sem.s4,
-                               src=T.res[8 * h + j], dst=T.res[8 * h + j]) for j in range(8)],
+            [RemoteDMATransfer(dst_ids=[did(ch, r) for r in ranks], dma_engine_mask=3 << (2 * j),
+                               remote_sem=T.sem.s4, srcs=[T.ag[j]], dsts=[T.res[8 * h + j] for r in ranks])
+             for j in range(8)],
             local_sem=T.sem.sent)
-        sent += 16
-        g.wait_ge(T.sem.s4, 16)
-        g.dma_start(T.y[:], T.res[:]).then_inc(T.sem.stored, 16)
-        g.wait_ge(T.sem.stored, 16)
-
-    if sent:
-        g.wait_ge(T.sem.sent, sent)
+        g.wait_ge(T.sem.sent, 16)

from concourse.bass import DstId, RemoteDMATransfer

UNITS = 16
SCRATCH = {
    "xs":  ("dram", [UNITS, 128, 8], "float32"),
    "pa":  ("dram", [UNITS, 128, 8], "float32"),
    "pb":  ("dram", [UNITS, 128, 8], "float32"),
    "rs":  ("dram", [8, 128, 8], "float32"),
    "ag":  ("dram", [8, 128, 8], "float32"),
    "res": ("dram", [UNITS, 128, 8], "float32"),
}
SEMAPHORES = ["loaded", "stored", "s1", "s2", "s3", "s4", "sent"]

PAIR = ((0, 3), (5, 6))
RELAY = (7, 4)


def rank_program(g, core, T, topo):
    ch, k = topo.chip(core), core % 8
    group = None
    for members in T.tables["GROUPS"]:
        cs = [T.cores[r] for r in members]
        if ch in [topo.chip(c) for c in cs]:
            group = cs
    if group is None:
        return
    chips = sorted(set(topo.chip(c) for c in group))
    me = chips.index(ch)
    ranks = sorted(c % 8 for c in group if topo.chip(c) == ch)
    assert len(chips) == 8 and len(ranks) == 2
    assert not set(ranks) & set(PAIR[0] + PAIR[1] + RELAY)

    def did(chip_, k_):
        rid, pid, _se = topo.addr(chip_ * 8 + k_)
        return DstId(rid=rid, pnc=pid)

    def sender(u):
        h, j = divmod(u, 8)
        return PAIR[h][j // 4]

    def reducer(u):
        h, j = divmod(u, 8)
        return PAIR[h][1 - j // 4]

    if k in ranks:
        g.sync.dma_start(T.xs[:], T.x[:]).then_inc(T.sem.loaded, 16)
        g.wait_ge(T.sem.loaded, 16)
        land = T.pa if k == ranks[0] else T.pb
        g.remote_dma_fused(
            [RemoteDMATransfer(dst_ids=[did(ch, sender(u))], dma_engine_mask=1 << u, remote_sem=T.sem.s1,
                               src=T.xs[u], dst=land[u]) for u in range(UNITS)],
            local_sem=T.sem.sent)
        g.sync.wait_ge(T.sem.s4, 32)
        g.sync.dma_start(T.y[:], T.res[:]).then_inc(T.sem.stored, 16)
        g.wait_ge(T.sem.sent, 16)
        g.wait_ge(T.sem.stored, 16)
        return

    if k in PAIR[0] + PAIR[1]:
        mine = [u for u in range(UNITS) if sender(u) == k]
        g.wait_ge(T.sem.s1, 8)
        g.remote_dma_fused(
            [RemoteDMATransfer(dst_ids=[did(chips[u % 8], reducer(u))], dma_engine_mask=3 << (2 * e),
                               remote_sem=T.sem.s2, srcs=[T.pa[u], T.pb[u]], dsts=[T.rs[me]], alu_op=1)
             for e, u in enumerate(mine)],
            local_sem=T.sem.sent)
        sent = 8
        red = [u for u in range(UNITS) if u % 8 == me and reducer(u) == k]
        for u in red:
            h = u // 8
            g.wait_ge(T.sem.s2, 16)
            g.remote_dma_fused(
                [RemoteDMATransfer(dst_ids=[did(c, RELAY[h]) for c in chips], dma_engine_mask=0xFF,
                                   remote_sem=T.sem.s3, srcs=[T.rs[i] for i in range(8)],
                                   dsts=[T.ag[me] for c in chips], alu_op=1)],
                local_sem=T.sem.sent)
            sent += 8
        g.wait_ge(T.sem.sent, sent)
        return

    if k in RELAY:
        h = RELAY.index(k)
        g.wait_ge(T.sem.s3, 64)
        g.remote_dma_fused(
            [RemoteDMATransfer(dst_ids=[did(ch, r) for r in ranks], dma_engine_mask=3 << (2 * j),
                               remote_sem=T.sem.s4, srcs=[T.ag[j]], dsts=[T.res[8 * h + j] for r in ranks])
             for j in range(8)],
            local_sem=T.sem.sent)
        g.wait_ge(T.sem.sent, 16)
